import numpy as np
import ml_dtypes


def mxq(x, axis, fmt="e4m3"):
    dtype, down = {"e4m3": (ml_dtypes.float8_e4m3fn, 7), "e5m2": (ml_dtypes.float8_e5m2, 14)}[fmt]
    v = np.moveaxis(np.asarray(x, np.float32).astype(ml_dtypes.bfloat16).astype(np.float64), axis, -1)
    blocks = v.reshape(v.shape[:-1] + (-1, 32))
    amax = np.abs(blocks).max(-1, keepdims=True)
    byte = np.maximum(np.where(amax > 0, np.frexp(amax)[1] - 1 + 127, 0) - down, 1)
    scale = np.exp2(byte - 127.0)
    codes = (blocks / scale).astype(np.float32).astype(dtype).astype(np.float64)
    return np.moveaxis((codes * scale).reshape(v.shape), -1, axis)


WIDE = False


def mx_kscale(k):
    if not WIDE:
        return np.ones(k)
    levels = np.array([10, -10, 5, -5, 0])
    if k % 512:
        return np.exp2(np.random.permutation(np.resize(levels, k // 32))).repeat(32)
    a = np.empty((k // 512, 16))
    for p in range(k // 512):
        a[p, :8] = np.random.permutation(np.resize(levels, 8))
        for g in range(8):
            far = levels[np.abs(levels - a[p, g]) >= 10]
            a[p, g + 8] = far[np.random.randint(len(far))]
    return np.exp2(a.ravel()).repeat(32)


def f64(x):
    return np.asarray(x).astype(np.float64)


def striped(idx):
    return np.tile(idx.reshape(-1, 16).T, (8, 1)).astype(np.uint16)


def unstriped(offs):
    return offs[:16].T.reshape(-1).astype(np.int64)


E2M1 = np.array([0.0, 0.5, 1.0, 1.5, 2.0, 3.0, 4.0, 6.0, -0.0, -0.5, -1.0, -1.5, -2.0, -3.0, -4.0, -6.0])


def pack_weight(w, fmt):
    k, n = w.shape
    w = f64(np.asarray(w, np.float32).astype(ml_dtypes.bfloat16)).reshape(k // 32, 32, n)
    amax = np.abs(w).max(1)
    if fmt == "e4m3":
        byte = np.frexp(amax)[1] - 1 + 127 - 7
    else:
        mant, ex = np.frexp(amax / 6.0)
        byte = np.where(mant > 0.5, ex, ex - 1) + 127
    byte = np.clip(np.where(amax > 0, byte, 1), 1, 254)
    scaled = (w * np.exp2(127.0 - byte)[:, None, :]).reshape(k, n).astype(np.float32)
    by_word = np.ascontiguousarray(scaled.reshape(k // 512, 128, 4, n).transpose(0, 1, 3, 2))
    if fmt == "e4m3":
        words = by_word.astype(ml_dtypes.float8_e4m3fn).view(np.uint8)
    else:
        c = by_word.astype(ml_dtypes.float4_e2m1fn).view(np.uint8) & 0xF
        words = (c[..., 0::2] | (c[..., 1::2] << 4)).reshape(k // 512, 128, 2 * n)
    return np.ascontiguousarray(words), np.ascontiguousarray(byte.astype(np.uint8).reshape(k // 512, 16, n))


def unpack_weight(words, scales, fmt):
    g, _, n = scales.shape
    words = np.ascontiguousarray(words).reshape(g, 128, n, -1)
    if fmt == "e4m3":
        vals = words.view(ml_dtypes.float8_e4m3fn).astype(np.float64)
    else:
        nib = np.empty((g, 128, n, 4), np.uint8)
        nib[..., 0::2] = words & 0xF
        nib[..., 1::2] = words >> 4
        vals = E2M1[nib]
    vals = vals * np.repeat(np.exp2(scales.astype(np.float64) - 127.0), 8, axis=1)[..., None]
    return vals.transpose(0, 1, 3, 2).reshape(g * 512, n)


def gelu(v):
    return 0.5 * v * (1.0 + np.tanh(np.sqrt(2.0 / np.pi) * (v + 0.044715 * v**3)))


K, K2, H, N, T, S = 1024, 512, 1024, 512, 2048, 1024

def setup_inputs():
    n = np.random.standard_normal
    s = mx_kscale(K)[:, None]
    s2 = mx_kscale(K2)[:, None]
    u = mx_kscale(H)[:, None]
    d = {}
    d["tab_words"], d["tab_scales"] = pack_weight(n((K, T)) * s, "e4m3")
    d["offs"] = striped(np.random.permutation(T)[:S])
    d["xs_words"], d["xs_scales"] = pack_weight(n((K2, S)) * s2, "e4m3")
    d["w1"] = (n((K, H)) / K**0.5 / s * u.T).astype(np.float32)
    d["w2"] = (n((K2, H)) / K2**0.5 / s2 * u.T).astype(np.float32)
    d["b2"] = (0.7 * n(H) * u[:, 0]).astype(np.float32)
    d["w3"] = (n((H, N)) / H**0.5 / u).astype(np.float32)
    d["w4_words"], d["w4_scales"] = pack_weight(n((H, N)) / H**0.5 / u, "e2m1")
    return d

def reference(tab_words, tab_scales, offs, xs_words, xs_scales, w1, w2, b2, w3, w4_words, w4_scales):
    v = unpack_weight(tab_words, tab_scales, "e4m3")[:, unstriped(offs)]
    xs = unpack_weight(xs_words, xs_scales, "e4m3")
    w4 = unpack_weight(w4_words, w4_scales, "e2m1")
    hist = mxq(f64(w1), 0, "e4m3").T @ v
    sens = (mxq(f64(w2), 0, "e4m3").T @ xs) + f64(b2)[:, None]
    total = mxq(hist + sens, 0, "e4m3")
    gap = mxq(np.abs(hist - sens), 0, "e4m3")
    y = mxq(f64(w3), 0, "e4m3").T @ total
    doubt = w4.T @ gap
    return y / (1.0 + np.abs(doubt))

@@ -1,0 +1,262 @@
+from contextlib import ExitStack
+
+import concourse.mybir as mybir
+
+K, K2, H, N, T, S = 1024, 512, 1024, 512, 2048, 1024
+FLOPS = 2 * S * (K * H + K2 * H + 2 * H * N)
+
+F32 = mybir.dt.float32
+BF16 = mybir.dt.bfloat16
+I32 = mybir.dt.int32
+U32 = mybir.dt.uint32
+U16 = mybir.dt.uint16
+U8 = mybir.dt.uint8
+FP8X4 = mybir.dt.float8_e4m3fn_x4
+FP4X4 = mybir.dt.float4_e2m1fn_x4
+ALU = mybir.AluOpType
+ACT = mybir.ActivationFunctionType
+
+P = 128
+PACK = 4
+KP = P * PACK
+JC = 128
+JH = 512
+LINE = 4
+
+
+def tile_list_oxygenator_clot_scores_kernel(
+    tc, tab_words, tab_scales, offs, xs_words, xs_scales, w1, w2, b2, w3, w4_words, w4_scales, out
+):
+    nc = tc.nc
+    with ExitStack() as ctx:
+        keep = ctx.enter_context(tc.tile_pool(name="keep", bufs=1))
+        ring = ctx.enter_context(tc.tile_pool(name="ring", bufs=3))
+        psum = ctx.enter_context(tc.psum_pool(name="psum", bufs=1))
+
+        offsets = keep.tile([P, S // 16], U16, name="offsets")
+        bias = keep.tile([P, 2, PACK], F32, name="bias")
+        tab_w = [keep.tile([P, T], I32, name=f"tab_w{g}") for g in range(2)]
+        tab_s = keep.tile([P, T], U8, name="tab_s", align_bytes=64)
+        xs_w = keep.tile([P, S], I32, name="xs_w", align_bytes=64)
+        xs_s = keep.tile([P, S], U8, name="xs_s", align_bytes=64)
+        w4_w = keep.tile([P, 2, 2 * N], U8, name="w4_w", align_bytes=64)
+        w4_s = keep.tile([P, 2, N], U8, name="w4_s", align_bytes=64)
+
+        warm = keep.tile([P, 1], F32, name="warm")
+        warmed = keep.tile([P, 1], F32, name="warmed")
+        nc.vector.memset(warm[:], 1.0)
+        nc.scalar.activation(out=warmed[:], in_=warm[:], func=ACT.Abs_reciprocal_sqrt)
+        nc.vector.memset(xs_s[:].bitcast(I32), 0)
+        nc.vector.memset(tab_s[:].bitcast(I32), 0)
+        nc.vector.memset(w4_s[:].rearrange("p a c -> p (a c)").bitcast(I32), 0)
+
+        raw = {}
+
+        def load_weight(name, w, g, a):
+            raw[name] = keep.tile([P, PACK, KP], F32, name=f"raw_{name}")
+            rows = w[g * KP : (g + 1) * KP, a * KP : (a + 1) * KP]
+            nc.sync.dma_start(out=raw[name][:], in_=rows.rearrange("(p j) c -> p j c", j=PACK))
+
+        def load_table(g):
+            nc.sync.dma_start(out=tab_w[g][:], in_=tab_words[g].rearrange("p t i -> p (t i)").bitcast(I32))
+
+        load_weight("w2_0", w2, 0, 0)
+        nc.sync.dma_start(out=xs_w[:], in_=xs_words[0].rearrange("p t i -> p (t i)").bitcast(I32))
+        for q in range(4):
+            nc.sync.dma_start(
+                out=xs_s[:].bitcast(I32)[32 * q : 32 * q + 4, :],
+                in_=xs_scales[0, 4 * q : 4 * q + 4, :].bitcast(I32),
+            )
+        nc.sync.dma_start(offsets[:], offs)
+        load_table(0)
+        nc.sync.dma_start(out=bias[:], in_=b2.rearrange("(a p t) -> p a t", a=2, t=PACK))
+        load_weight("w1_00", w1, 0, 0)
+        for q in range(4):
+            nc.sync.dma_start(
+                out=tab_s[:].bitcast(I32)[32 * q : 32 * q + 8, :],
+                in_=tab_scales[:, 4 * q : 4 * q + 4, :].bitcast(I32),
+            )
+        load_table(1)
+        load_weight("w1_01", w1, 1, 0)
+        load_weight("w2_1", w2, 0, 1)
+        load_weight("w1_10", w1, 0, 1)
+        load_weight("w1_11", w1, 1, 1)
+        load_weight("w3_0", w3, 0, 0)
+        load_weight("w3_1", w3, 1, 0)
+        nc.sync.dma_start(out=w4_w[:].bitcast(I32), in_=w4_words.rearrange("a p c -> p a c").bitcast(I32))
+        for q in range(4):
+            nc.sync.dma_start(
+                out=w4_s[:].bitcast(I32)[32 * q : 32 * q + 4, :, :],
+                in_=w4_scales[:, 4 * q : 4 * q + 4, :].rearrange("a r c -> r a c").bitcast(I32),
+            )
+
+        codes = {}
+        scales = {}
+
+        def prepare(name, dealt, engines):
+            grouped = ring.tile([P, KP * PACK], BF16, name="grouped", align_bytes=64)
+            if dealt:
+                src = raw[name][:].rearrange("p j (m t) -> p m j t", t=PACK)
+                dst = grouped[:].rearrange("p (t m j) -> p m j t", t=PACK, j=PACK)
+            else:
+                src = raw[name][:].rearrange("p j (m i) -> p m j i", i=LINE)
+                dst = grouped[:].rearrange("p (m i j) -> p m j i", i=LINE, j=PACK)
+            for half, engine in enumerate(engines):
+                m = slice(half * P // 2, (half + 1) * P // 2)
+                if engine == "V":
+                    nc.vector.tensor_copy(out=dst[:, m], in_=src[:, m])
+                else:
+                    nc.scalar.copy(out=dst[:, m], in_=src[:, m])
+            codes[name] = keep.tile([P, KP], U32, name=f"codes_{name}", align_bytes=64)
+            scales[name] = keep.tile([P, KP], U8, name=f"scales_{name}", align_bytes=64)
+            nc.vector.quantize_mx(out=codes[name][:].bitcast(FP8X4), scales=scales[name][:], in_=grouped[:])
+
+        v_w = {}
+        v_s = {}
+
+        def gather_words(g, jh):
+            v_w[g, jh] = keep.tile([P, JH], U32, name=f"v_w{g}{jh}", align_bytes=64)
+            picks = offsets[:, jh * JH // 16 : (jh + 1) * JH // 16]
+            nc.vector.tensor_copy(v_w[g, jh][:], tab_w[g][:].bitcast(U32).indirect(picks))
+
+        def gather_scales(jh):
+            v_s[jh] = keep.tile([P, JH], U8, name=f"v_s{jh}", align_bytes=64)
+            picks = offsets[:, jh * JH // 16 : (jh + 1) * JH // 16]
+            nc.vector.tensor_copy(v_s[jh][:], tab_s[:].indirect(picks))
+
+        sens = {}
+
+        def make_sens(a, jh):
+            sens[a, jh] = keep.tile([P, JH // LINE, PACK, LINE], F32, name=f"sens{a}{jh}")
+            cols = slice(jh * JH, (jh + 1) * JH)
+            name = f"w2_{a}"
+            for t in range(PACK):
+                bank = psum.tile([P, JH], F32, name="bank_sd", bufs=3)
+                nc.tensor.matmul_mx(
+                    out=bank[:],
+                    lhsT=codes[name][:, t * P : (t + 1) * P].bitcast(FP8X4),
+                    lhsT_scale=scales[name][:, t * P : (t + 1) * P],
+                    rhs=xs_w[:, cols].bitcast(FP8X4),
+                    rhs_scale=xs_s[:, cols],
+                    start=True,
+                    stop=True,
+                )
+                nc.scalar.activation(
+                    out=sens[a, jh][:, :, t, :],
+                    in_=bank[:].rearrange("p (c i) -> p c i", i=LINE),
+                    func=ACT.Identity,
+                    bias=bias[:, a, t : t + 1],
+                )
+
+        tg_codes = {}
+        tg_scales = {}
+
+        def first_stage(a, jc):
+            jh, j0 = divmod(jc * JC, JH)
+            cols = slice(j0, j0 + JC)
+            bank = psum.tile([P, PACK, JC], F32, name="bank_h", bufs=3)
+            for t in range(PACK):
+                for g in range(2):
+                    name = f"w1_{a}{g}"
+                    nc.tensor.matmul_mx(
+                        out=bank[:, t, :],
+                        lhsT=codes[name][:, t * P : (t + 1) * P].bitcast(FP8X4),
+                        lhsT_scale=scales[name][:, t * P : (t + 1) * P],
+                        rhs=v_w[g, jh][:, cols].bitcast(FP8X4),
+                        rhs_scale=v_s[jh][4 * g : P, cols],
+                        start=(g == 0),
+                        stop=(g == 1),
+                    )
+            hist = bank[:].rearrange("p t (c i) -> p c t i", i=LINE)
+            sens_c = sens[a, jh][:, j0 // LINE : (j0 + JC) // LINE]
+            pair = ring.tile([P, 2, JC * PACK], BF16, name="pair", align_bytes=64)
+            diff = ring.tile([P, JC * PACK], BF16, name="diff")
+            nc.vector.tensor_tensor(
+                out=diff[:].rearrange("p (c i t) -> p c t i", i=LINE, t=PACK), in0=hist, in1=sens_c, op=ALU.subtract
+            )
+            nc.vector.tensor_tensor(
+                out=pair[:, 0, :].rearrange("p (c i t) -> p c t i", i=LINE, t=PACK), in0=hist, in1=sens_c, op=ALU.add
+            )
+            nc.scalar.activation(out=pair[:, 1, :], in_=diff[:], func=ACT.Abs)
+            tg_codes[a, jc] = keep.tile([P, 2 * JC], U32, name=f"tg_codes{a}{jc}", align_bytes=64)
+            tg_scales[a, jc] = keep.tile([P, 2 * JC], U8, name=f"tg_scales{a}{jc}", align_bytes=64)
+            nc.vector.quantize_mx(
+                out=tg_codes[a, jc][:].bitcast(FP8X4),
+                scales=tg_scales[a, jc][:],
+                in_=pair[:].rearrange("p h c -> p (h c)"),
+            )
+
+        def second_stage(jc, on_vector):
+            doubt = psum.tile([P, N // P, JC], F32, name="bank_sd", bufs=3)
+            y = psum.tile([P, N // P, JC], F32, name="bank_y", bufs=2)
+            for n in range(N // P):
+                for a in range(2):
+                    nc.tensor.matmul_mx(
+                        out=doubt[:, n, :],
+                        lhsT=w4_w[:, a, 2 * n * P : 2 * (n + 1) * P].bitcast(FP4X4),
+                        lhsT_scale=w4_s[:, a, n * P : (n + 1) * P],
+                        rhs=tg_codes[a, jc][:, JC:].bitcast(FP8X4),
+                        rhs_scale=tg_scales[a, jc][:, JC:],
+                        start=(a == 0),
+                        stop=(a == 1),
+                    )
+            for n in range(N // P):
+                for a in range(2):
+                    nc.tensor.matmul_mx(
+                        out=y[:, n, :],
+                        lhsT=codes[f"w3_{a}"][:, n * P : (n + 1) * P].bitcast(FP8X4),
+                        lhsT_scale=scales[f"w3_{a}"][:, n * P : (n + 1) * P],
+                        rhs=tg_codes[a, jc][:, :JC].bitcast(FP8X4),
+                        rhs_scale=tg_scales[a, jc][:, :JC],
+                        start=(a == 0),
+                        stop=(a == 1),
+                    )
+            size = ring.tile([P, N // P, JC], F32, name="size")
+            squared = ring.tile([P, N // P, JC], F32, name="squared")
+            damp = ring.tile([P, N // P, JC], F32, name="damp")
+            result = ring.tile([P, N // P, JC], F32, name="result")
+            nc.scalar.activation(out=size[:], in_=doubt[:], func=ACT.Abs)
+            if on_vector:
+                nc.vector.scalar_tensor_tensor(
+                    out=squared[:], in0=size[:], scalar=2.0, in1=size[:], op0=ALU.add, op1=ALU.mult
+                )
+                nc.scalar.activation(out=damp[:], in_=squared[:], func=ACT.Abs_reciprocal_sqrt, bias=1.0)
+            else:
+                nc.scalar.activation(out=squared[:], in_=size[:], func=ACT.Square, bias=1.0)
+                nc.scalar.activation(out=damp[:], in_=squared[:], func=ACT.Abs_reciprocal_sqrt)
+            nc.vector.tensor_tensor(out=result[:], in0=y[:], in1=damp[:], op=ALU.mult)
+            nc.sync.dma_start(
+                out=out[:, jc * JC : (jc + 1) * JC].rearrange("(n p) j -> p n j", p=P), in_=result[:]
+            )
+
+        prepare("w2_0", True, "SV")
+        make_sens(0, 0)
+        gather_words(0, 0)
+        gather_words(0, 1)
+        make_sens(0, 1)
+        prepare("w1_00", True, "SS")
+        gather_scales(0)
+        gather_words(1, 0)
+        prepare("w1_01", True, "SV")
+        gather_scales(1)
+        gather_words(1, 1)
+        for jc in range(S // JC):
+            first_stage(0, jc)
+            if jc == 0:
+                prepare("w2_1", True, "SS")
+            if jc == 1:
+                prepare("w1_10", True, "SS")
+            if jc == 3:
+                prepare("w1_11", True, "SV")
+                make_sens(1, 0)
+            if jc == 5:
+                prepare("w3_0", False, "SV")
+            if jc == 6:
+                make_sens(1, 1)
+            if jc == 7:
+                prepare("w3_1", False, "VV")
+        for jc in range(S // JC + 2):
+            if jc < S // JC:
+                first_stage(1, jc)
+            if jc > 1:
+                second_stage(jc - 2, jc - 2 >= 5)

@@ -18,10 +18,16 @@ ACT = mybir.ActivationFunctionType
 
 P = 128
 PACK = 4
-KP = P * PACK
-JC = 128
-JH = 512
-LINE = 4
+PASS = P * PACK
+QUAD = 32
+BANK = 512
+CHUNK = BANK // PACK
+CHUNKS = S // CHUNK
+N_TILES = N // P
+PAIR = 2
+ALIGN = 64
+RING = 3
+HIST_BANKS, SENS_DOUBT_BANKS, Y_BANKS = 3, 3, 2
 
 
 def tile_list_oxygenator_clot_scores_kernel(
@@ -30,193 +36,179 @@ def tile_list_oxygenator_clot_scores_kernel(
     nc = tc.nc
     with ExitStack() as ctx:
         keep = ctx.enter_context(tc.tile_pool(name="keep", bufs=1))
-        ring = ctx.enter_context(tc.tile_pool(name="ring", bufs=3))
+        ring = ctx.enter_context(tc.tile_pool(name="ring", bufs=RING))
         psum = ctx.enter_context(tc.psum_pool(name="psum", bufs=1))
 
         offsets = keep.tile([P, S // 16], U16, name="offsets")
-        bias = keep.tile([P, 2, PACK], F32, name="bias")
-        tab_w = [keep.tile([P, T], I32, name=f"tab_w{g}") for g in range(2)]
-        tab_s = keep.tile([P, T], U8, name="tab_s", align_bytes=64)
-        xs_w = keep.tile([P, S], I32, name="xs_w", align_bytes=64)
-        xs_s = keep.tile([P, S], U8, name="xs_s", align_bytes=64)
-        w4_w = keep.tile([P, 2, 2 * N], U8, name="w4_w", align_bytes=64)
-        w4_s = keep.tile([P, 2, N], U8, name="w4_s", align_bytes=64)
+        bias = keep.tile([P, H // PASS, PACK], F32, name="bias")
+        table = [keep.tile([P, T], I32, name=f"table{g}") for g in range(K // PASS)]
+        table_plane = keep.tile([P, T], U8, name="table_plane", align_bytes=ALIGN)
+        xs_tile = keep.tile([P, S], I32, name="xs_tile", align_bytes=ALIGN)
+        xs_plane = keep.tile([P, S], U8, name="xs_plane", align_bytes=ALIGN)
+        w4_tile = keep.tile([P, H // PASS, 2 * N], U8, name="w4_tile", align_bytes=ALIGN)
+        w4_plane = keep.tile([P, H // PASS * N], U8, name="w4_plane", align_bytes=ALIGN)
 
-        warm = keep.tile([P, 1], F32, name="warm")
-        warmed = keep.tile([P, 1], F32, name="warmed")
-        nc.vector.memset(warm[:], 1.0)
-        nc.scalar.activation(out=warmed[:], in_=warm[:], func=ACT.Abs_reciprocal_sqrt)
-        nc.vector.memset(xs_s[:].bitcast(I32), 0)
-        nc.vector.memset(tab_s[:].bitcast(I32), 0)
-        nc.vector.memset(w4_s[:].rearrange("p a c -> p (a c)").bitcast(I32), 0)
+        nc.vector.memset(table_plane[:].bitcast(I32), 0)
+        nc.vector.memset(xs_plane[:].bitcast(I32), 0)
+        warm_in = keep.tile([P, 1], F32, name="warm_in")
+        warm_out = keep.tile([P, 1], F32, name="warm_out")
+        nc.vector.memset(warm_in[:], 1.0)
+        nc.scalar.activation(out=warm_out[:], in_=warm_in[:], func=ACT.Abs_reciprocal_sqrt)
+        nc.vector.memset(w4_plane[:].bitcast(I32), 0)
 
         raw = {}
 
         def load_weight(name, w, g, a):
-            raw[name] = keep.tile([P, PACK, KP], F32, name=f"raw_{name}")
-            rows = w[g * KP : (g + 1) * KP, a * KP : (a + 1) * KP]
-            nc.sync.dma_start(out=raw[name][:], in_=rows.rearrange("(p j) c -> p j c", j=PACK))
+            raw[name, g, a] = keep.tile([P, PACK, PASS], F32, name=f"raw_{name}{g}{a}")
+            rows = w[g * PASS : (g + 1) * PASS, a * PASS : (a + 1) * PASS]
+            nc.sync.dma_start(out=raw[name, g, a][:], in_=rows.rearrange("(p t) c -> p t c", t=PACK))
 
-        def load_table(g):
-            nc.sync.dma_start(out=tab_w[g][:], in_=tab_words[g].rearrange("p t i -> p (t i)").bitcast(I32))
+        def load_words(tile, words):
+            nc.sync.dma_start(out=tile[:], in_=words.rearrange("p c t -> p (c t)").bitcast(I32))
 
-        load_weight("w2_0", w2, 0, 0)
-        nc.sync.dma_start(out=xs_w[:], in_=xs_words[0].rearrange("p t i -> p (t i)").bitcast(I32))
-        for q in range(4):
-            nc.sync.dma_start(
-                out=xs_s[:].bitcast(I32)[32 * q : 32 * q + 4, :],
-                in_=xs_scales[0, 4 * q : 4 * q + 4, :].bitcast(I32),
-            )
+        def load_plane(plane, scale_rows, first_row):
+            for quad in range(P // QUAD):
+                p0 = quad * QUAD + first_row
+                nc.sync.dma_start(
+                    out=plane[:].bitcast(I32)[p0 : p0 + PACK, :],
+                    in_=scale_rows[quad * PACK : (quad + 1) * PACK].bitcast(I32),
+                )
+
+        load_plane(table_plane, tab_scales[0], 0)
+        load_weight("w2", w2, 0, 0)
         nc.sync.dma_start(offsets[:], offs)
-        load_table(0)
-        nc.sync.dma_start(out=bias[:], in_=b2.rearrange("(a p t) -> p a t", a=2, t=PACK))
-        load_weight("w1_00", w1, 0, 0)
-        for q in range(4):
-            nc.sync.dma_start(
-                out=tab_s[:].bitcast(I32)[32 * q : 32 * q + 8, :],
-                in_=tab_scales[:, 4 * q : 4 * q + 4, :].bitcast(I32),
-            )
-        load_table(1)
-        load_weight("w1_01", w1, 1, 0)
-        load_weight("w2_1", w2, 0, 1)
-        load_weight("w1_10", w1, 0, 1)
-        load_weight("w1_11", w1, 1, 1)
-        load_weight("w3_0", w3, 0, 0)
-        load_weight("w3_1", w3, 1, 0)
-        nc.sync.dma_start(out=w4_w[:].bitcast(I32), in_=w4_words.rearrange("a p c -> p a c").bitcast(I32))
-        for q in range(4):
-            nc.sync.dma_start(
-                out=w4_s[:].bitcast(I32)[32 * q : 32 * q + 4, :, :],
-                in_=w4_scales[:, 4 * q : 4 * q + 4, :].rearrange("a r c -> r a c").bitcast(I32),
-            )
+        load_plane(table_plane, tab_scales[1], PACK)
+        load_words(table[0], tab_words[0])
+        load_words(xs_tile, xs_words[0])
+        load_plane(xs_plane, xs_scales[0], 0)
+        nc.sync.dma_start(out=bias[:], in_=b2.rearrange("(a p t) -> p a t", p=P, t=PACK))
+        load_weight("w2", w2, 0, 1)
+        load_words(table[1], tab_words[1])
+        for a in range(H // PASS):
+            for g in range(K // PASS):
+                load_weight("w1", w1, g, a)
+        load_weight("w3", w3, 0, 0)
+        nc.sync.dma_start(out=w4_tile[:].bitcast(I32), in_=w4_words.rearrange("a p c -> p a c").bitcast(I32))
+        load_plane(w4_plane, w4_scales.rearrange("a q c -> q a c"), 0)
+        load_weight("w3", w3, 1, 0)
 
-        codes = {}
-        scales = {}
+        def quantize(source, name):
+            columns = source.shape[1] // PACK
+            words = keep.tile([P, columns], U32, name=f"words_{name}", align_bytes=ALIGN)
+            plane = keep.tile([P, columns], U8, name=f"plane_{name}", align_bytes=ALIGN)
+            nc.vector.quantize_mx(out=words[:].bitcast(FP8X4), scales=plane[:], in_=source)
+            return words, plane
 
-        def prepare(name, dealt, engines):
-            grouped = ring.tile([P, KP * PACK], BF16, name="grouped", align_bytes=64)
-            if dealt:
-                src = raw[name][:].rearrange("p j (m t) -> p m j t", t=PACK)
-                dst = grouped[:].rearrange("p (t m j) -> p m j t", t=PACK, j=PACK)
+        weights = {}
+
+        def quantize_weight(name, g, a, copies):
+            rounded = ring.tile([P, PASS * PACK], BF16, name="rounded", align_bytes=ALIGN)
+            if name == "w3":
+                src = raw[name, g, a][:].rearrange("p t (h m i) -> p h m t i", h=2, i=PAIR)
+                dst = rounded[:].rearrange("p (h m i t) -> p h m t i", h=2, i=PAIR, t=PACK)
             else:
-                src = raw[name][:].rearrange("p j (m i) -> p m j i", i=LINE)
-                dst = grouped[:].rearrange("p (m i j) -> p m j i", i=LINE, j=PACK)
-            for half, engine in enumerate(engines):
-                m = slice(half * P // 2, (half + 1) * P // 2)
-                if engine == "V":
-                    nc.vector.tensor_copy(out=dst[:, m], in_=src[:, m])
-                else:
-                    nc.scalar.copy(out=dst[:, m], in_=src[:, m])
-            codes[name] = keep.tile([P, KP], U32, name=f"codes_{name}", align_bytes=64)
-            scales[name] = keep.tile([P, KP], U8, name=f"scales_{name}", align_bytes=64)
-            nc.vector.quantize_mx(out=codes[name][:].bitcast(FP8X4), scales=scales[name][:], in_=grouped[:])
+                src = raw[name, g, a][:].rearrange("p t (m h i) -> p h m t i", h=2, i=PAIR)
+                dst = rounded[:].rearrange("p (h i m t) -> p h m t i", h=2, i=PAIR, t=PACK)
+            for h, copy in enumerate(copies):
+                copy(out=dst[:, h], in_=src[:, h])
+            weights[name, g, a] = quantize(rounded[:], f"{name}{g}{a}")
 
-        v_w = {}
-        v_s = {}
+        def stationary(name, g, a, tile):
+            words, plane = weights[name, g, a]
+            columns = slice(tile * P, (tile + 1) * P)
+            return dict(lhsT=words[:, columns].bitcast(FP8X4), lhsT_scale=plane[:, columns])
 
-        def gather_words(g, jh):
-            v_w[g, jh] = keep.tile([P, JH], U32, name=f"v_w{g}{jh}", align_bytes=64)
-            picks = offsets[:, jh * JH // 16 : (jh + 1) * JH // 16]
-            nc.vector.tensor_copy(v_w[g, jh][:], tab_w[g][:].bitcast(U32).indirect(picks))
+        picked = {}
 
-        def gather_scales(jh):
-            v_s[jh] = keep.tile([P, JH], U8, name=f"v_s{jh}", align_bytes=64)
-            picks = offsets[:, jh * JH // 16 : (jh + 1) * JH // 16]
-            nc.vector.tensor_copy(v_s[jh][:], tab_s[:].indirect(picks))
+        def gather_words(g):
+            picked[g] = keep.tile([P, S], U32, name=f"picked{g}", align_bytes=ALIGN)
+            nc.vector.tensor_copy(picked[g][:], table[g][:].bitcast(U32).indirect(offsets[:]))
 
         sens = {}
 
-        def make_sens(a, jh):
-            sens[a, jh] = keep.tile([P, JH // LINE, PACK, LINE], F32, name=f"sens{a}{jh}")
-            cols = slice(jh * JH, (jh + 1) * JH)
-            name = f"w2_{a}"
-            for t in range(PACK):
-                bank = psum.tile([P, JH], F32, name="bank_sd", bufs=3)
-                nc.tensor.matmul_mx(
-                    out=bank[:],
-                    lhsT=codes[name][:, t * P : (t + 1) * P].bitcast(FP8X4),
-                    lhsT_scale=scales[name][:, t * P : (t + 1) * P],
-                    rhs=xs_w[:, cols].bitcast(FP8X4),
-                    rhs_scale=xs_s[:, cols],
-                    start=True,
-                    stop=True,
-                )
-                nc.scalar.activation(
-                    out=sens[a, jh][:, :, t, :],
-                    in_=bank[:].rearrange("p (c i) -> p c i", i=LINE),
-                    func=ACT.Identity,
-                    bias=bias[:, a, t : t + 1],
-                )
+        def make_sens(a):
+            for half in range(S // BANK):
+                sens[a, half] = keep.tile([P, PACK, BANK], F32, name=f"sens{a}{half}")
+                entries = slice(half * BANK, (half + 1) * BANK)
+                for t in range(PACK):
+                    bank = psum.tile([P, BANK], F32, name="sens_doubt", bufs=SENS_DOUBT_BANKS)
+                    nc.tensor.matmul_mx(
+                        out=bank[:],
+                        **stationary("w2", 0, a, t),
+                        rhs=xs_tile[:, entries].bitcast(FP8X4),
+                        rhs_scale=xs_plane[:, entries],
+                        start=True,
+                        stop=True,
+                    )
+                    nc.scalar.activation(
+                        out=sens[a, half][:, t, :], in_=bank[:], func=ACT.Identity, bias=bias[:, a, t : t + 1]
+                    )
 
-        tg_codes = {}
-        tg_scales = {}
+        total_mx = {}
+        gap_mx = {}
 
-        def first_stage(a, jc):
-            jh, j0 = divmod(jc * JC, JH)
-            cols = slice(j0, j0 + JC)
-            bank = psum.tile([P, PACK, JC], F32, name="bank_h", bufs=3)
-            for t in range(PACK):
-                for g in range(2):
-                    name = f"w1_{a}{g}"
+        def first_stage(a, chunk):
+            entries = slice(chunk * CHUNK, (chunk + 1) * CHUNK)
+            bank = psum.tile([P, PACK, CHUNK], F32, name="hist", bufs=HIST_BANKS)
+            for g in range(K // PASS):
+                for t in range(PACK):
                     nc.tensor.matmul_mx(
                         out=bank[:, t, :],
-                        lhsT=codes[name][:, t * P : (t + 1) * P].bitcast(FP8X4),
-                        lhsT_scale=scales[name][:, t * P : (t + 1) * P],
-                        rhs=v_w[g, jh][:, cols].bitcast(FP8X4),
-                        rhs_scale=v_s[jh][4 * g : P, cols],
-                        start=(g == 0),
-                        stop=(g == 1),
+                        **stationary("w1", g, a, t),
+                        rhs=picked[g][:, entries].bitcast(FP8X4),
+                        rhs_scale=picked_plane[g * PACK :, entries],
+                        start=(g == 0 and t == 0),
+                        stop=(g == K // PASS - 1 and t == PACK - 1),
                     )
-            hist = bank[:].rearrange("p t (c i) -> p c t i", i=LINE)
-            sens_c = sens[a, jh][:, j0 // LINE : (j0 + JC) // LINE]
-            pair = ring.tile([P, 2, JC * PACK], BF16, name="pair", align_bytes=64)
-            diff = ring.tile([P, JC * PACK], BF16, name="diff")
-            nc.vector.tensor_tensor(
-                out=diff[:].rearrange("p (c i t) -> p c t i", i=LINE, t=PACK), in0=hist, in1=sens_c, op=ALU.subtract
-            )
-            nc.vector.tensor_tensor(
-                out=pair[:, 0, :].rearrange("p (c i t) -> p c t i", i=LINE, t=PACK), in0=hist, in1=sens_c, op=ALU.add
-            )
-            nc.scalar.activation(out=pair[:, 1, :], in_=diff[:], func=ACT.Abs)
-            tg_codes[a, jc] = keep.tile([P, 2 * JC], U32, name=f"tg_codes{a}{jc}", align_bytes=64)
-            tg_scales[a, jc] = keep.tile([P, 2 * JC], U8, name=f"tg_scales{a}{jc}", align_bytes=64)
-            nc.vector.quantize_mx(
-                out=tg_codes[a, jc][:].bitcast(FP8X4),
-                scales=tg_scales[a, jc][:],
-                in_=pair[:].rearrange("p h c -> p (h c)"),
+            half, j0 = divmod(chunk * CHUNK, BANK)
+            hist_in = bank[:].rearrange("p t (c i) -> p c t i", i=PAIR)
+            sens_in = sens[a, half][:, :, j0 : j0 + CHUNK].rearrange("p t (c i) -> p c t i", i=PAIR)
+            both = ring.tile([P, 2, CHUNK * PACK], BF16, name="both", align_bytes=ALIGN)
+            diff = ring.tile([P, CHUNK * PACK], BF16, name="diff")
+            for dst, op in ((diff[:], ALU.subtract), (both[:, 0, :], ALU.add)):
+                nc.vector.tensor_tensor(
+                    out=dst.rearrange("p (c i t) -> p c t i", i=PAIR, t=PACK), in0=hist_in, in1=sens_in, op=op
+                )
+            nc.scalar.activation(out=both[:, 1, :], in_=diff[:], func=ACT.Abs)
+            if (a, chunk) == (H // PASS - 1, CHUNKS - 1):
+                gap_mx[a, chunk] = quantize(both[:, 1, :], "last_gap")
+                total_mx[a, chunk] = quantize(both[:, 0, :], "last_total")
+            else:
+                words, plane = quantize(both[:].rearrange("p h c -> p (h c)"), f"both{a}{chunk}")
+                total_mx[a, chunk] = (words[:, :CHUNK], plane[:, :CHUNK])
+                gap_mx[a, chunk] = (words[:, CHUNK:], plane[:, CHUNK:])
+
+        def product_over_r(bank, tiles, stationary_of, moving, chunk):
+            for a in range(H // PASS):
+                words, plane = moving[a, chunk]
+                for c, n in enumerate(tiles):
+                    nc.tensor.matmul_mx(
+                        out=bank[:, c, :],
+                        **stationary_of(a, n),
+                        rhs=words[:].bitcast(FP8X4),
+                        rhs_scale=plane[:],
+                        start=(a == 0 and c == 0),
+                        stop=(a == H // PASS - 1 and c == len(tiles) - 1),
+                    )
+
+        def w4_operand(a, n):
+            return dict(
+                lhsT=w4_tile[:, a, 2 * n * P : 2 * (n + 1) * P].bitcast(FP4X4),
+                lhsT_scale=w4_plane[:, a * N + n * P : a * N + (n + 1) * P],
             )
 
-        def second_stage(jc, on_vector):
-            doubt = psum.tile([P, N // P, JC], F32, name="bank_sd", bufs=3)
-            y = psum.tile([P, N // P, JC], F32, name="bank_y", bufs=2)
-            for n in range(N // P):
-                for a in range(2):
-                    nc.tensor.matmul_mx(
-                        out=doubt[:, n, :],
-                        lhsT=w4_w[:, a, 2 * n * P : 2 * (n + 1) * P].bitcast(FP4X4),
-                        lhsT_scale=w4_s[:, a, n * P : (n + 1) * P],
-                        rhs=tg_codes[a, jc][:, JC:].bitcast(FP8X4),
-                        rhs_scale=tg_scales[a, jc][:, JC:],
-                        start=(a == 0),
-                        stop=(a == 1),
-                    )
-            for n in range(N // P):
-                for a in range(2):
-                    nc.tensor.matmul_mx(
-                        out=y[:, n, :],
-                        lhsT=codes[f"w3_{a}"][:, n * P : (n + 1) * P].bitcast(FP8X4),
-                        lhsT_scale=scales[f"w3_{a}"][:, n * P : (n + 1) * P],
-                        rhs=tg_codes[a, jc][:, :JC].bitcast(FP8X4),
-                        rhs_scale=tg_scales[a, jc][:, :JC],
-                        start=(a == 0),
-                        stop=(a == 1),
-                    )
-            size = ring.tile([P, N // P, JC], F32, name="size")
-            squared = ring.tile([P, N // P, JC], F32, name="squared")
-            damp = ring.tile([P, N // P, JC], F32, name="damp")
-            result = ring.tile([P, N // P, JC], F32, name="result")
+        def second_stage(chunk, tiles, square_on_vector):
+            shape = [P, len(tiles), CHUNK]
+            size = ring.tile(shape, F32, name="size")
+            squared = ring.tile(shape, F32, name="squared")
+            damp = ring.tile(shape, F32, name="damp")
+            result = ring.tile(shape, F32, name="result")
+            doubt = psum.tile(shape, F32, name="sens_doubt", bufs=SENS_DOUBT_BANKS)
+            product_over_r(doubt, tiles, w4_operand, gap_mx, chunk)
             nc.scalar.activation(out=size[:], in_=doubt[:], func=ACT.Abs)
-            if on_vector:
+            y = psum.tile(shape, F32, name="y", bufs=Y_BANKS)
+            product_over_r(y, tiles, lambda a, n: stationary("w3", a, 0, n), total_mx, chunk)
+            if square_on_vector:
                 nc.vector.scalar_tensor_tensor(
                     out=squared[:], in0=size[:], scalar=2.0, in1=size[:], op0=ALU.add, op1=ALU.mult
                 )
@@ -225,38 +217,34 @@ def tile_list_oxygenator_clot_scores_kernel(
                 nc.scalar.activation(out=squared[:], in_=size[:], func=ACT.Square, bias=1.0)
                 nc.scalar.activation(out=damp[:], in_=squared[:], func=ACT.Abs_reciprocal_sqrt)
             nc.vector.tensor_tensor(out=result[:], in0=y[:], in1=damp[:], op=ALU.mult)
-            nc.sync.dma_start(
-                out=out[:, jc * JC : (jc + 1) * JC].rearrange("(n p) j -> p n j", p=P), in_=result[:]
-            )
+            rows = out[tiles[0] * P : (tiles[-1] + 1) * P, chunk * CHUNK : (chunk + 1) * CHUNK]
+            nc.sync.dma_start(out=rows.rearrange("(n p) j -> p n j", p=P), in_=result[:])
 
-        prepare("w2_0", True, "SV")
-        make_sens(0, 0)
-        gather_words(0, 0)
-        gather_words(0, 1)
-        make_sens(0, 1)
-        prepare("w1_00", True, "SS")
-        gather_scales(0)
-        gather_words(1, 0)
-        prepare("w1_01", True, "SV")
-        gather_scales(1)
-        gather_words(1, 1)
-        for jc in range(S // JC):
-            first_stage(0, jc)
-            if jc == 0:
-                prepare("w2_1", True, "SS")
-            if jc == 1:
-                prepare("w1_10", True, "SS")
-            if jc == 3:
-                prepare("w1_11", True, "SV")
-                make_sens(1, 0)
-            if jc == 5:
-                prepare("w3_0", False, "SV")
-            if jc == 6:
-                make_sens(1, 1)
-            if jc == 7:
-                prepare("w3_1", False, "VV")
-        for jc in range(S // JC + 2):
-            if jc < S // JC:
-                first_stage(1, jc)
-            if jc > 1:
-                second_stage(jc - 2, jc - 2 >= 5)
+        on_scalar, on_vector = nc.scalar.copy, nc.vector.tensor_copy
+
+        picked_plane = keep.tile([P, S], U8, name="picked_plane", align_bytes=ALIGN)
+        nc.vector.tensor_copy(picked_plane[:], table_plane[:].indirect(offsets[:]))
+        quantize_weight("w2", 0, 0, (on_scalar, on_vector))
+        make_sens(0)
+        gather_words(0)
+        quantize_weight("w2", 0, 1, (on_vector, on_vector))
+        make_sens(1)
+        gather_words(1)
+        for g in range(K // PASS):
+            quantize_weight("w1", g, 0, (on_vector, on_vector))
+
+        late_pieces = [("w1", 0, 1), ("w1", 1, 1), ("w3", 0, 0), ("w3", 1, 0)]
+        for chunk, piece in enumerate(late_pieces):
+            first_stage(0, chunk)
+            quantize_weight(*piece, (on_scalar, on_scalar))
+
+        completed = None
+        for chunk in range(CHUNKS):
+            for a in range(H // PASS):
+                if (a, chunk) not in total_mx:
+                    first_stage(a, chunk)
+                    if completed is not None:
+                        second_stage(completed, range(N_TILES), False)
+                    completed = chunk if a == H // PASS - 1 and chunk < CHUNKS - 1 else None
+        for n0 in range(0, N_TILES, N_TILES // 2):
+            second_stage(CHUNKS - 1, range(n0, n0 + N_TILES // 2), True)

from contextlib import ExitStack

import concourse.mybir as mybir

K, K2, H, N, T, S = 1024, 512, 1024, 512, 2048, 1024
FLOPS = 2 * S * (K * H + K2 * H + 2 * H * N)

F32 = mybir.dt.float32
BF16 = mybir.dt.bfloat16
I32 = mybir.dt.int32
U32 = mybir.dt.uint32
U16 = mybir.dt.uint16
U8 = mybir.dt.uint8
FP8X4 = mybir.dt.float8_e4m3fn_x4
FP4X4 = mybir.dt.float4_e2m1fn_x4
ALU = mybir.AluOpType
ACT = mybir.ActivationFunctionType

P = 128
PACK = 4
PASS = P * PACK
QUAD = 32
BANK = 512
CHUNK = BANK // PACK
CHUNKS = S // CHUNK
N_TILES = N // P
PAIR = 2
ALIGN = 64
RING = 3
HIST_BANKS, SENS_DOUBT_BANKS, Y_BANKS = 3, 3, 2


def tile_list_oxygenator_clot_scores_kernel(
    tc, tab_words, tab_scales, offs, xs_words, xs_scales, w1, w2, b2, w3, w4_words, w4_scales, out
):
    nc = tc.nc
    with ExitStack() as ctx:
        keep = ctx.enter_context(tc.tile_pool(name="keep", bufs=1))
        ring = ctx.enter_context(tc.tile_pool(name="ring", bufs=RING))
        psum = ctx.enter_context(tc.psum_pool(name="psum", bufs=1))

        offsets = keep.tile([P, S // 16], U16, name="offsets")
        bias = keep.tile([P, H // PASS, PACK], F32, name="bias")
        table = [keep.tile([P, T], I32, name=f"table{g}") for g in range(K // PASS)]
        table_plane = keep.tile([P, T], U8, name="table_plane", align_bytes=ALIGN)
        xs_tile = keep.tile([P, S], I32, name="xs_tile", align_bytes=ALIGN)
        xs_plane = keep.tile([P, S], U8, name="xs_plane", align_bytes=ALIGN)
        w4_tile = keep.tile([P, H // PASS, 2 * N], U8, name="w4_tile", align_bytes=ALIGN)
        w4_plane = keep.tile([P, H // PASS * N], U8, name="w4_plane", align_bytes=ALIGN)

        nc.vector.memset(table_plane[:].bitcast(I32), 0)
        nc.vector.memset(xs_plane[:].bitcast(I32), 0)
        warm_in = keep.tile([P, 1], F32, name="warm_in")
        warm_out = keep.tile([P, 1], F32, name="warm_out")
        nc.vector.memset(warm_in[:], 1.0)
        nc.scalar.activation(out=warm_out[:], in_=warm_in[:], func=ACT.Abs_reciprocal_sqrt)
        nc.vector.memset(w4_plane[:].bitcast(I32), 0)

        raw = {}

        def load_weight(name, w, g, a):
            raw[name, g, a] = keep.tile([P, PACK, PASS], F32, name=f"raw_{name}{g}{a}")
            rows = w[g * PASS : (g + 1) * PASS, a * PASS : (a + 1) * PASS]
            nc.sync.dma_start(out=raw[name, g, a][:], in_=rows.rearrange("(p t) c -> p t c", t=PACK))

        def load_words(tile, words):
            nc.sync.dma_start(out=tile[:], in_=words.rearrange("p c t -> p (c t)").bitcast(I32))

        def load_plane(plane, scale_rows, first_row):
            for quad in range(P // QUAD):
                p0 = quad * QUAD + first_row
                nc.sync.dma_start(
                    out=plane[:].bitcast(I32)[p0 : p0 + PACK, :],
                    in_=scale_rows[quad * PACK : (quad + 1) * PACK].bitcast(I32),
                )

        load_plane(table_plane, tab_scales[0], 0)
        load_weight("w2", w2, 0, 0)
        nc.sync.dma_start(offsets[:], offs)
        load_plane(table_plane, tab_scales[1], PACK)
        load_words(table[0], tab_words[0])
        load_words(xs_tile, xs_words[0])
        load_plane(xs_plane, xs_scales[0], 0)
        nc.sync.dma_start(out=bias[:], in_=b2.rearrange("(a p t) -> p a t", p=P, t=PACK))
        load_weight("w2", w2, 0, 1)
        load_words(table[1], tab_words[1])
        for a in range(H // PASS):
            for g in range(K // PASS):
                load_weight("w1", w1, g, a)
        load_weight("w3", w3, 0, 0)
        nc.sync.dma_start(out=w4_tile[:].bitcast(I32), in_=w4_words.rearrange("a p c -> p a c").bitcast(I32))
        load_plane(w4_plane, w4_scales.rearrange("a q c -> q a c"), 0)
        load_weight("w3", w3, 1, 0)

        def quantize(source, name):
            columns = source.shape[1] // PACK
            words = keep.tile([P, columns], U32, name=f"words_{name}", align_bytes=ALIGN)
            plane = keep.tile([P, columns], U8, name=f"plane_{name}", align_bytes=ALIGN)
            nc.vector.quantize_mx(out=words[:].bitcast(FP8X4), scales=plane[:], in_=source)
            return words, plane

        weights = {}

        def quantize_weight(name, g, a, copies):
            rounded = ring.tile([P, PASS * PACK], BF16, name="rounded", align_bytes=ALIGN)
            if name == "w3":
                src = raw[name, g, a][:].rearrange("p t (h m i) -> p h m t i", h=2, i=PAIR)
                dst = rounded[:].rearrange("p (h m i t) -> p h m t i", h=2, i=PAIR, t=PACK)
            else:
                src = raw[name, g, a][:].rearrange("p t (m h i) -> p h m t i", h=2, i=PAIR)
                dst = rounded[:].rearrange("p (h i m t) -> p h m t i", h=2, i=PAIR, t=PACK)
            for h, copy in enumerate(copies):
                copy(out=dst[:, h], in_=src[:, h])
            weights[name, g, a] = quantize(rounded[:], f"{name}{g}{a}")

        def stationary(name, g, a, tile):
            words, plane = weights[name, g, a]
            columns = slice(tile * P, (tile + 1) * P)
            return dict(lhsT=words[:, columns].bitcast(FP8X4), lhsT_scale=plane[:, columns])

        picked = {}

        def gather_words(g):
            picked[g] = keep.tile([P, S], U32, name=f"picked{g}", align_bytes=ALIGN)
            nc.vector.tensor_copy(picked[g][:], table[g][:].bitcast(U32).indirect(offsets[:]))

        sens = {}

        def make_sens(a):
            for half in range(S // BANK):
                sens[a, half] = keep.tile([P, PACK, BANK], F32, name=f"sens{a}{half}")
                entries = slice(half * BANK, (half + 1) * BANK)
                for t in range(PACK):
                    bank = psum.tile([P, BANK], F32, name="sens_doubt", bufs=SENS_DOUBT_BANKS)
                    nc.tensor.matmul_mx(
                        out=bank[:],
                        **stationary("w2", 0, a, t),
                        rhs=xs_tile[:, entries].bitcast(FP8X4),
                        rhs_scale=xs_plane[:, entries],
                        start=True,
                        stop=True,
                    )
                    nc.scalar.activation(
                        out=sens[a, half][:, t, :], in_=bank[:], func=ACT.Identity, bias=bias[:, a, t : t + 1]
                    )

        total_mx = {}
        gap_mx = {}

        def first_stage(a, chunk):
            entries = slice(chunk * CHUNK, (chunk + 1) * CHUNK)
            bank = psum.tile([P, PACK, CHUNK], F32, name="hist", bufs=HIST_BANKS)
            for g in range(K // PASS):
                for t in range(PACK):
                    nc.tensor.matmul_mx(
                        out=bank[:, t, :],
                        **stationary("w1", g, a, t),
                        rhs=picked[g][:, entries].bitcast(FP8X4),
                        rhs_scale=picked_plane[g * PACK :, entries],
                        start=(g == 0 and t == 0),
                        stop=(g == K // PASS - 1 and t == PACK - 1),
                    )
            half, j0 = divmod(chunk * CHUNK, BANK)
            hist_in = bank[:].rearrange("p t (c i) -> p c t i", i=PAIR)
            sens_in = sens[a, half][:, :, j0 : j0 + CHUNK].rearrange("p t (c i) -> p c t i", i=PAIR)
            both = ring.tile([P, 2, CHUNK * PACK], BF16, name="both", align_bytes=ALIGN)
            diff = ring.tile([P, CHUNK * PACK], BF16, name="diff")
            for dst, op in ((diff[:], ALU.subtract), (both[:, 0, :], ALU.add)):
                nc.vector.tensor_tensor(
                    out=dst.rearrange("p (c i t) -> p c t i", i=PAIR, t=PACK), in0=hist_in, in1=sens_in, op=op
                )
            nc.scalar.activation(out=both[:, 1, :], in_=diff[:], func=ACT.Abs)
            if (a, chunk) == (H // PASS - 1, CHUNKS - 1):
                gap_mx[a, chunk] = quantize(both[:, 1, :], "last_gap")
                total_mx[a, chunk] = quantize(both[:, 0, :], "last_total")
            else:
                words, plane = quantize(both[:].rearrange("p h c -> p (h c)"), f"both{a}{chunk}")
                total_mx[a, chunk] = (words[:, :CHUNK], plane[:, :CHUNK])
                gap_mx[a, chunk] = (words[:, CHUNK:], plane[:, CHUNK:])

        def product_over_r(bank, tiles, stationary_of, moving, chunk):
            for a in range(H // PASS):
                words, plane = moving[a, chunk]
                for c, n in enumerate(tiles):
                    nc.tensor.matmul_mx(
                        out=bank[:, c, :],
                        **stationary_of(a, n),
                        rhs=words[:].bitcast(FP8X4),
                        rhs_scale=plane[:],
                        start=(a == 0 and c == 0),
                        stop=(a == H // PASS - 1 and c == len(tiles) - 1),
                    )

        def w4_operand(a, n):
            return dict(
                lhsT=w4_tile[:, a, 2 * n * P : 2 * (n + 1) * P].bitcast(FP4X4),
                lhsT_scale=w4_plane[:, a * N + n * P : a * N + (n + 1) * P],
            )

        def second_stage(chunk, tiles, square_on_vector):
            shape = [P, len(tiles), CHUNK]
            size = ring.tile(shape, F32, name="size")
            squared = ring.tile(shape, F32, name="squared")
            damp = ring.tile(shape, F32, name="damp")
            result = ring.tile(shape, F32, name="result")
            doubt = psum.tile(shape, F32, name="sens_doubt", bufs=SENS_DOUBT_BANKS)
            product_over_r(doubt, tiles, w4_operand, gap_mx, chunk)
            nc.scalar.activation(out=size[:], in_=doubt[:], func=ACT.Abs)
            y = psum.tile(shape, F32, name="y", bufs=Y_BANKS)
            product_over_r(y, tiles, lambda a, n: stationary("w3", a, 0, n), total_mx, chunk)
            if square_on_vector:
                nc.vector.scalar_tensor_tensor(
                    out=squared[:], in0=size[:], scalar=2.0, in1=size[:], op0=ALU.add, op1=ALU.mult
                )
                nc.scalar.activation(out=damp[:], in_=squared[:], func=ACT.Abs_reciprocal_sqrt, bias=1.0)
            else:
                nc.scalar.activation(out=squared[:], in_=size[:], func=ACT.Square, bias=1.0)
                nc.scalar.activation(out=damp[:], in_=squared[:], func=ACT.Abs_reciprocal_sqrt)
            nc.vector.tensor_tensor(out=result[:], in0=y[:], in1=damp[:], op=ALU.mult)
            rows = out[tiles[0] * P : (tiles[-1] + 1) * P, chunk * CHUNK : (chunk + 1) * CHUNK]
            nc.sync.dma_start(out=rows.rearrange("(n p) j -> p n j", p=P), in_=result[:])

        on_scalar, on_vector = nc.scalar.copy, nc.vector.tensor_copy

        picked_plane = keep.tile([P, S], U8, name="picked_plane", align_bytes=ALIGN)
        nc.vector.tensor_copy(picked_plane[:], table_plane[:].indirect(offsets[:]))
        quantize_weight("w2", 0, 0, (on_scalar, on_vector))
        make_sens(0)
        gather_words(0)
        quantize_weight("w2", 0, 1, (on_vector, on_vector))
        make_sens(1)
        gather_words(1)
        for g in range(K // PASS):
            quantize_weight("w1", g, 0, (on_vector, on_vector))

        late_pieces = [("w1", 0, 1), ("w1", 1, 1), ("w3", 0, 0), ("w3", 1, 0)]
        for chunk, piece in enumerate(late_pieces):
            first_stage(0, chunk)
            quantize_weight(*piece, (on_scalar, on_scalar))

        completed = None
        for chunk in range(CHUNKS):
            for a in range(H // PASS):
                if (a, chunk) not in total_mx:
                    first_stage(a, chunk)
                    if completed is not None:
                        second_stage(completed, range(N_TILES), False)
                    completed = chunk if a == H // PASS - 1 and chunk < CHUNKS - 1 else None
        for n0 in range(0, N_TILES, N_TILES // 2):
            second_stage(CHUNKS - 1, range(n0, n0 + N_TILES // 2), True)
